import numpy as np, ml_dtypes
CORES = [76,84,92,100,108,116,124]
N = 7
import mx_ref
NC, G = 256, 4
C = np.float32(2.0 ** -5)
CNT = [[16,8,120,0,32,72,8],[48,0,48,0,32,112,16],[8,16,40,32,160,0,0],[104,72,0,8,0,24,48],[0,0,16,40,0,48,152],[40,8,32,136,8,0,32],[40,152,0,40,24,0,0]]
OFF = [[sum(c[:e]) for e in range(N + 1)] for c in CNT]
BF = ml_dtypes.bfloat16
def cut(t, i, w=512):
    return t[:, w * i:w * i + w]
def tile(rs):
    return np.stack(rs, axis=2).reshape(128, -1).astype(BF)
def layer(w, X):
    out = []
    for i in range(G):
        for t in range(len(X)):
            p = mx_ref.matmul(mx_ref.quantize(cut(w, len(X) * i + t)), X[t])
            z = p if t == 0 else z + p
        out.append(z)
    return out
def gated(Z, g):
    return [(np.maximum(z, 0) * C) * g for z in Z]
def setup_inputs(rng):
    def f(*shape):
        return mx_ref.flush((rng.standard_normal(shape, dtype=np.float32) * np.exp2(rng.integers(-2, 3, shape[:-1] + (1,)))).astype(BF))
    gt = np.broadcast_to((0.125 + 0.875 * rng.random((N, 1, NC))).astype(BF), (N, 128, NC)).copy()
    return {"gt": gt, "x": f(N, 128, 4 * NC), "w1": f(N, 128, G * 512), "w2": f(N, 128, 512)}
def setup_inputs_blocks(rng):
    d = setup_inputs(rng)
    for k in ("x", "w1", "w2"): d[k] = mx_ref.spread(d[k], rng, 4)
    return d
def setup_inputs_wide(rng):
    d = setup_inputs(rng)
    for k in ("x", "w1", "w2"): d[k] = mx_ref.flush((d[k].astype(np.float32) * np.exp2(rng.integers(-8, 9, (N, 1, 1))).astype(np.float32)).astype(BF))
    return d
def setup_inputs_zeros(rng):
    d = setup_inputs(rng); v = d["x"].reshape(N, 128, -1, 4).copy()
    v[np.broadcast_to((rng.random((N, 1, v.shape[2], 1)) < 0.33), v.shape)] = 0
    d["x"] = v.reshape(d["x"].shape)
    return d
def reference(gt, x, w1, w2):
    y = np.zeros((N, 128, NC), np.float32)
    for e in range(N):
        t = np.concatenate([x[j][:, 4 * OFF[j][e]:4 * OFF[j][e + 1]] for j in range(N)], axis=1)
        g = np.concatenate([gt[j][:, OFF[j][e]:OFF[j][e + 1]] for j in range(N)], axis=1).astype(np.float32)
        y[e] = mx_ref.matmul(mx_ref.quantize(w2[e]), mx_ref.quantize(tile(gated(layer(w1[e], [mx_ref.quantize(t)]), g))))
    return {"y": y}

@@ -1,0 +1,349 @@
+from concourse.bass import DstId, RemoteDMATransfer
+from concourse.mybir import dt, AluOpType, ActivationFunctionType
+
+NR = 7
+NCOL = 256
+HALF = 128
+LW = 400
+
+SCRATCH = {
+    "xt": ("sbuf", [128, 4 * NCOL], "bfloat16"),
+    "w1t": ("sbuf", [128, 2048], "bfloat16"),
+    "w2t": ("sbuf", [128, 512], "bfloat16"),
+    "xq": ("sbuf", [128, NCOL], "float8_e4m3fn_x4"),
+    "xs": ("sbuf", [128, NCOL], "uint8"),
+    "w1q": ("sbuf", [128, 512], "float8_e4m3fn_x4"),
+    "w1s": ("sbuf", [128, 512], "uint8"),
+    "w2q": ("sbuf", [128, 128], "float8_e4m3fn_x4"),
+    "w2s": ("sbuf", [128, 128], "uint8"),
+    "fc": ("sbuf", [128, NCOL], "float8_e4m3fn_x4"),
+    "fs": ("sbuf", [128, NCOL], "uint8"),
+    "L": ("sbuf", [128, LW], "float8_e4m3fn_x4"),
+    "P": ("sbuf", [128, LW], "uint8"),
+    "gd": ("dram", [128, 2], "bfloat16"),
+    "gl": ("dram", [NR, 128, 2], "bfloat16"),
+    "gr": ("sbuf", [128, NCOL], "bfloat16"),
+    "G": ("sbuf", [128, NCOL], "bfloat16"),
+    "h0": ("sbuf", [128, 512], "bfloat16"),
+    "h1": ("sbuf", [128, 512], "bfloat16"),
+    "hq0": ("sbuf", [128, 128], "float8_e4m3fn_x4"),
+    "hq1": ("sbuf", [128, 128], "float8_e4m3fn_x4"),
+    "hs0": ("sbuf", [128, 128], "uint8"),
+    "hs1": ("sbuf", [128, 128], "uint8"),
+    "ys": ("sbuf", [128, NCOL], "float32"),
+    "zp": ("psum", [128, 512 * 8], "float32"),
+}
+SEMAPHORES = ["ldx", "ldg", "ldw1", "ldw2", "qx", "qo", "qw1", "qw2", "sent",
+              "fcs",
+              "g0", "g1", "a0", "a1",
+              "lg0", "lg1", "bg0", "bg1",
+              "mm", "tt", "rl", "qh0", "qh1", "my0", "my1", "cp", "st"]
+
+ENG_RELAY = 8
+ENG_OFF = 8
+
+
+def off(cnt, j, e):
+    return sum(cnt[j][:e])
+
+
+def engines(topo, src, dsts, k, part=0):
+    m = -1
+    for d in dsts:
+        m &= topo.mask(src, d)
+    bits = [i for i in range(m.bit_length()) if (m >> i) & 1]
+    return sum(1 << i for i in bits[part * k:part * k + k])
+
+
+def plan(T, topo):
+    cnt, cores = T.tables["CNT"], T.cores
+    roads = []
+    for j in range(NR):
+        me = cores[j]
+        dests = [e for e in range(NR) if e != j and cnt[j][e]]
+        near = [e for e in dests if topo.may_write(me, cores[e])]
+        far = [e for e in dests if e not in near]
+        near.sort(key=lambda e: -cnt[j][e])
+        mates = [c for c in range(me - 8, me + 8)
+                 if c >= 0 and c != me and topo.chip(c) == topo.chip(me) and all(topo.may_write(c, cores[e]) for e in far)]
+        here = [c for c in mates if topo.die(c) == topo.die(me)]
+        there = [c for c in mates if topo.die(c) != topo.die(me)]
+        groups = [far[:2], far[2:]] if len(far) > 2 else [far]
+        gates = {}
+        who = []
+        for k, grp in enumerate(groups):
+            who.append((here[k], there[k]))
+            gates[here[k]] = grp[0]
+            gates[there[k]] = grp[1]
+        if len(near) > 2:
+            groups[0] = groups[0] + [near.pop()]
+        wins = [(min(off(cnt, j, e) for e in grp), max(off(cnt, j, e + 1) for e in grp)) for grp in groups]
+        w = max(b - a for a, b in wins)
+        wins = [(min(a, NCOL - w), min(a, NCOL - w) + w) for a, b in wins]
+        calls = []
+        for grp in groups:
+            widths = sorted(set(cnt[j][e] for e in grp), reverse=True)
+            calls.append([[e for e in grp if cnt[j][e] == n] for n in widths])
+        roads.append({"near": near, "groups": groups, "who": who, "gates": gates, "wins": wins, "calls": calls})
+    return roads
+
+
+def arrivals(roads, cnt, e):
+    out = []
+    for j in range(NR):
+        if j == e or not cnt[j][e]:
+            continue
+        r = roads[j]
+        if e in r["near"]:
+            out.append((r["near"].index(e), j, ENG_OFF))
+        else:
+            for calls in r["calls"]:
+                for i, c in enumerate(calls):
+                    if e in c:
+                        out.append((2 + i, j, ENG_OFF // len(c)))
+    return sorted(out)
+
+
+def layout(roads, cnt, e):
+    own = cnt[e][e]
+    arr = arrivals(roads, cnt, e)
+    eng = {j: k for _, j, k in arr}
+    first, cut, fill = [], None, own
+    rest = [j for _, j, _ in arr]
+    while fill < HALF:
+        j = rest.pop(0)
+        fill += cnt[j][e]
+        if fill <= HALF:
+            first.append(j)
+        else:
+            cut = j
+    first.sort()
+    rest.sort()
+    o_end = off(cnt, e, e + 1)
+    mid = [] if cut is None else [cut]
+    if own and o_end < HALF:
+        seq = rest + mid + first + [e]
+        start = (own - NCOL) % 16
+        q_at, q_from = start + NCOL - own, off(cnt, e, e)
+        lo_first = False
+    else:
+        seq = ([e] if own else []) + first + mid + rest
+        start = HALF - own
+        q_at, q_from = 0, o_end - HALF
+        lo_first = True
+    pos, p = {}, start
+    for j in seq:
+        pos[j] = p
+        p += cnt[j][e]
+    base = (start, start + HALF) if lo_first else (start + HALF, start)
+    group = {j: 0 if j in first or j == cut else 1 for j in eng}
+    need = [sum(2 * eng[j] for j in eng if group[j] == h) for h in (0, 1)]
+    return {"pos": pos, "start": start, "base": base, "group": group, "need": need, "own": own,
+            "q_at": q_at, "q_from": q_from, "seq": seq}
+
+
+def gate_targets(T, roads, lays, j):
+    by = {"g0": [(h, T.gd[:, :]) for h in sorted(roads[j]["gates"])]}
+    for e in range(NR):
+        if j in lays[e]["group"] and e not in roads[j]["gates"].values():
+            by.setdefault("g%d" % lays[e]["group"][j], []).append((T.cores[e], T.gl[j]))
+    return by
+
+
+def send_gates(g, core, T, topo, by):
+    k = ENG_OFF // len(by)
+    everyone = [c for name in by for c, _ in by[name]]
+    trs = []
+    for i, name in enumerate(sorted(by)):
+        ids = []
+        for c, _ in by[name]:
+            rid, pid, _ = topo.addr(c)
+            ids.append(DstId(rid=rid, pnc=pid))
+        trs.append(RemoteDMATransfer(dst_ids=ids, dma_engine_mask=engines(topo, core, everyone, k, i),
+                                     remote_sem=T.sem[name], srcs=[T.gd[:, :]], dsts=[d for _, d in by[name]]))
+    g.remote_dma_fused(trs, local_sem=T.sem.sent)
+    return k * len(by)
+
+
+def send_runs(g, core, T, topo, cnt, lays, j, dests, kind, src, shift):
+    k = ENG_OFF // len(dests)
+    parts = []
+    for i, e in enumerate(dests):
+        lay = lays[e]
+        n, o, p = cnt[j][e], off(cnt, j, e) - shift, lay["pos"][j]
+        if kind == 0:
+            dst, s = T.L[:, p:p + n].bitcast(dt.uint8), src[:, o:o + n].bitcast(dt.uint8)
+        else:
+            dst, s = T.P[:, p:p + n], src[:, o:o + n]
+        parts.append((T.cores[e], dst, s, T.sem["a%d" % lay["group"][j]], engines(topo, core, [T.cores[e]], k, i)))
+    send(g, T, topo, parts)
+    return k * len(dests)
+
+
+def send(g, T, topo, parts):
+    if len(parts) == 1:
+        c, dst, s, sem, m = parts[0]
+        rid, pid, _ = topo.addr(c)
+        g.remote_dma(dst, s, sem, T.sem.sent, pid, rid, m)
+        return
+    trs = []
+    for c, dst, s, sem, m in parts:
+        rid, pid, _ = topo.addr(c)
+        trs.append(RemoteDMATransfer(dst_ids=[DstId(rid=rid, pnc=pid)], dma_engine_mask=m, remote_sem=sem,
+                                     srcs=[s], dsts=[dst]))
+    g.remote_dma_fused(trs, local_sem=T.sem.sent)
+
+
+def relay(g, core, T, topo, r, kind):
+    k = ENG_RELAY // len(r["groups"])
+    parts = []
+    for i, pair in enumerate(r["who"]):
+        a, b = r["wins"][i]
+        if kind == 0:
+            dst, s = T.fc[:, 0:b - a].bitcast(dt.uint8), T.xq[:, a:b].bitcast(dt.uint8)
+        else:
+            dst, s = T.fs[:, 0:b - a], T.xs[:, a:b]
+        parts.append((pair[kind], dst, s, T.sem.fcs, engines(topo, core, [pair[kind]], k, i)))
+    send(g, T, topo, parts)
+    return k * len(parts)
+
+
+def rank_program(g, core, T, topo):
+    cnt = T.tables["CNT"]
+    roads = plan(T, topo)
+    lays = [layout(roads, cnt, e) for e in range(NR)]
+    rank = T.rank_of(core)
+    if rank is not None:
+        rank_core(g, core, T, topo, cnt, roads, lays, rank)
+        return
+    for j in range(NR):
+        for k, pair in enumerate(roads[j]["who"]):
+            if core in pair:
+                helper_core(g, core, T, topo, cnt, roads, lays, j, k, pair.index(core))
+
+
+def helper_core(g, core, T, topo, cnt, roads, lays, j, k, kind):
+    r = roads[j]
+    e = r["gates"][core]
+    g.wait_ge(T.sem.g0, ENG_OFF // len(gate_targets(T, roads, lays, j)))
+    total = send_gates(g, core, T, topo, {"g%d" % lays[e]["group"][j]: [(T.cores[e], T.gl[j])]})
+    src = T.fc if kind == 0 else T.fs
+    g.wait_ge(T.sem.fcs, ENG_RELAY // len(r["groups"]))
+    for dests in r["calls"][k]:
+        total += send_runs(g, core, T, topo, cnt, lays, j, dests, kind, src, r["wins"][k][0])
+    g.wait_ge(T.sem.sent, total)
+
+
+def rank_core(g, core, T, topo, cnt, roads, lays, rank):
+    S = T.sem
+    r = roads[rank]
+    lay = lays[rank]
+    own, start = lay["own"], lay["start"]
+    V, A, Y, PE = g.vector, g.scalar, g.sync, g.tensor
+
+    Y.dma_start(T.xt[:, :], T.x[:, :]).then_inc(S.ldx, 16)
+    A.dma_start(T.gd[:, :], T.gt[0:1, :]).then_inc(S.ldg, 16)
+    Y.dma_start(T.w1t[:, :], T.w1[:, :]).then_inc(S.ldw1, 16)
+    Y.dma_start(T.w2t[:, :], T.w2[:, :]).then_inc(S.ldw2, 16)
+
+    V.wait_ge(S.ldx, 16)
+    V.quantize_mx(T.xq[:, :], T.xs[:, :], T.xt[:, :]).then_inc(S.qx, 1)
+    if own:
+        a, c = lay["q_at"], lay["q_from"]
+        V.quantize_mx(T.L[:, a:a + HALF], T.P[:, a:a + HALF], T.xt[:, 4 * c:4 * (c + HALF)]).then_inc(S.qo, 1)
+    V.wait_ge(S.ldw1, 16)
+    V.quantize_mx(T.w1q[:, :], T.w1s[:, :], T.w1t[:, :]).then_inc(S.qw1, 1)
+    V.wait_ge(S.ldw2, 16)
+    V.quantize_mx(T.w2q[:, :], T.w2s[:, :], T.w2t[:, :]).then_inc(S.qw2, 1)
+
+    g.wait_ge(S.ldg, 16)
+    total = send_gates(g, core, T, topo, gate_targets(T, roads, lays, rank))
+    g.wait_ge(S.qx, 1)
+    total += relay(g, core, T, topo, r, 0)
+    total += relay(g, core, T, topo, r, 1)
+    for e in r["near"]:
+        total += send_runs(g, core, T, topo, cnt, lays, rank, [e], 0, T.xq, 0)
+        total += send_runs(g, core, T, topo, cnt, lays, rank, [e], 1, T.xs, 0)
+
+    for h, q in ((0, Y), (1, A)):
+        srcs = sorted(j for j in lay["group"] if lay["group"][j] == h)
+        n = 0
+        if h == 0 and own:
+            p, o = lay["pos"][rank] - start, off(cnt, rank, rank)
+            q.dma_start(T.gr[0:1, p:p + own], T.gt[0:1, o:o + own]).then_inc(S["lg%d" % h], 16)
+            n += 16
+        if srcs:
+            adds = [ENG_OFF if rank in roads[j]["gates"].values() else ENG_OFF // len(gate_targets(T, roads, lays, j))
+                    for j in srcs]
+            q.wait_ge(S["g%d" % h], sum(adds))
+        for j in srcs:
+            p, o, w = lay["pos"][j] - start, off(cnt, j, rank), cnt[j][rank]
+            q.dma_start(T.gr[0:1, p:p + w], T.gl[j, o // 2:(o + w) // 2, :]).then_inc(S["lg%d" % h], 16)
+            n += 16
+    for h in (0, 1):
+        n = 16 * sum(1 for j in lay["seq"] if lay["group"].get(j, 0) == h)
+        c = lay["base"][h] - start
+        if n:
+            g.wait_ge(S["lg%d" % h], n)
+        g.partition_broadcast(T.G[:, c:c + HALF], T.gr[0:1, c:c + HALF], 128).then_inc(S["bg%d" % h], 1)
+
+    PE.wait_ge(S.qw1, 1)
+    if own:
+        PE.wait_ge(S.qo, 1)
+    for h in (0, 1):
+        if lay["need"][h]:
+            PE.wait_ge(S["a%d" % h], lay["need"][h])
+        c = lay["base"][h]
+        for b in range(4):
+            z = 512 * (4 * h + b)
+            PE.matmul_mx(T.zp[:, z:z + HALF], T.w1q[:, 128 * b:128 * b + 128], T.w1s[:, 128 * b:128 * b + 128],
+                         T.L[:, c:c + HALF], T.P[:, c:c + HALF], True, True).then_inc(S.mm, 1)
+    PE.wait_ge(S.qw2, 1)
+    for h in (0, 1):
+        PE.wait_ge(S["qh%d" % h], 1)
+        PE.matmul_mx(T.zp[:, 2048 * h:2048 * h + HALF], T.w2q[:, :], T.w2s[:, :],
+                     T["hq%d" % h][:, :], T["hs%d" % h][:, :], True, True).then_inc(S["my%d" % h], 1)
+
+    for h in (0, 1):
+        c = lay["base"][h] - start
+        hb = T["h%d" % h]
+        V.wait_ge(S["bg%d" % h], 1)
+        for b in range(4):
+            z = 512 * (4 * h + b)
+            V.wait_ge(S.mm, 4 * h + b + 1)
+            V.tensor_tensor(hb[:, b:512:4], T.zp[:, z:z + HALF], T.G[:, c:c + HALF], AluOpType.mult).then_inc(S.tt, 1)
+        V.wait_ge(S.tt, 4 * h + 4)
+        V.tensor_scalar(hb[:, :], hb[:, :], 0.0, 2.0 ** -5, AluOpType.max, AluOpType.mult).then_inc(S.rl, 1)
+        V.wait_ge(S.rl, h + 1)
+        V.quantize_mx(T["hq%d" % h][:, :], T["hs%d" % h][:, :], hb[:, :]).then_inc(S["qh%d" % h], 1)
+
+    ypos, p = {}, 0
+    for j in range(NR):
+        ypos[j] = p
+        p += cnt[j][rank]
+    copies = 0
+    for h in (0, 1):
+        lo = lay["base"][h]
+        segs = []
+        for j in lay["seq"]:
+            a = max(lay["pos"][j], lo)
+            b = min(lay["pos"][j] + cnt[j][rank], lo + HALF)
+            if a >= b:
+                continue
+            to = ypos[j] + a - lay["pos"][j]
+            if segs and segs[-1][1] + segs[-1][2] == to:
+                segs[-1][2] += b - a
+            else:
+                segs.append([a - lo, to, b - a])
+        (A if h == 0 else V).wait_ge(S["my%d" % h], 1)
+        for a, to, n in segs:
+            src, dst = T.zp[:, 2048 * h + a:2048 * h + a + n], T.ys[:, to:to + n]
+            if h == 0:
+                A.activation(dst, src, ActivationFunctionType.Copy).then_inc(S.cp, 1)
+            else:
+                V.tensor_copy(dst, src).then_inc(S.cp, 1)
+            copies += 1
+    Y.wait_ge(S.cp, copies)
+    Y.dma_start(T.y[:, :], T.ys[:, :]).then_inc(S.st, 16)
+    Y.wait_ge(S.st, 16)
+    g.wait_ge(S.sent, total)

@@ -34,13 +34,13 @@ SCRATCH = {
     "zp": ("psum", [128, 512 * 8], "float32"),
 }
 SEMAPHORES = ["ldx", "ldg", "ldw1", "ldw2", "qx", "qo", "qw1", "qw2", "sent",
-              "fcs",
-              "g0", "g1", "a0", "a1",
-              "lg0", "lg1", "bg0", "bg1",
-              "mm", "tt", "rl", "qh0", "qh1", "my0", "my1", "cp", "st"]
+              "gh", "fcs",
+              "gn", "gf", "a0", "a1",
+              "lgn", "lgf", "bg",
+              "mm", "tt", "rv", "ra", "qh0", "qh1", "my0", "my1", "cp", "st"]
 
-ENG_RELAY = 8
-ENG_OFF = 8
+ENG = 8
+ENG_GH = 1
 
 
 def off(cnt, j, e):
@@ -75,6 +75,7 @@ def plan(T, topo):
             who.append((here[k], there[k]))
             gates[here[k]] = grp[0]
             gates[there[k]] = grp[1]
+        direct = list(near)
         if len(near) > 2:
             groups[0] = groups[0] + [near.pop()]
         wins = [(min(off(cnt, j, e) for e in grp), max(off(cnt, j, e + 1) for e in grp)) for grp in groups]
@@ -84,7 +85,8 @@ def plan(T, topo):
         for grp in groups:
             widths = sorted(set(cnt[j][e] for e in grp), reverse=True)
             calls.append([[e for e in grp if cnt[j][e] == n] for n in widths])
-        roads.append({"near": near, "groups": groups, "who": who, "gates": gates, "wins": wins, "calls": calls})
+        roads.append({"near": near, "groups": groups, "who": who, "gates": gates, "direct": direct, "wins": wins,
+                      "calls": calls})
     return roads
 
 
@@ -95,13 +97,17 @@ def arrivals(roads, cnt, e):
             continue
         r = roads[j]
         if e in r["near"]:
-            out.append((r["near"].index(e), j, ENG_OFF))
+            out.append((r["near"].index(e), j, ENG))
         else:
             for calls in r["calls"]:
                 for i, c in enumerate(calls):
                     if e in c:
-                        out.append((2 + i, j, ENG_OFF // len(c)))
+                        out.append((2 + i, j, ENG // len(c)))
     return sorted(out)
+
+
+def orders(js):
+    return [[]] if not js else [[j] + o for j in js for o in orders([i for i in js if i != j])]
 
 
 def layout(roads, cnt, e):
@@ -117,67 +123,51 @@ def layout(roads, cnt, e):
             first.append(j)
         else:
             cut = j
-    first.sort()
-    rest.sort()
-    o_end = off(cnt, e, e + 1)
+    direct = [j for j in eng if e in roads[j]["direct"]]
     mid = [] if cut is None else [cut]
-    if own and o_end < HALF:
-        seq = rest + mid + first + [e]
-        start = (own - NCOL) % 16
-        q_at, q_from = start + NCOL - own, off(cnt, e, e)
-        lo_first = False
-    else:
-        seq = ([e] if own else []) + first + mid + rest
+    ranks = [j for j in range(NR) if cnt[j][e]]
+    nxt = {a: b for a, b in zip(ranks, ranks[1:])}
+    o_end = off(cnt, e, e + 1)
+    lo_first = not (own and o_end < HALF)
+    first.sort(key=lambda j: (j not in direct, j))
+    best = None
+    for a in orders([j for j in rest if j in direct]):
+        for b in orders([j for j in rest if j not in direct]):
+            s = mid + a + b if lo_first else b + a + mid
+            joins = sum(1 for i, j in zip(s, s[1:]) if nxt.get(i) == j)
+            if best is None or joins > best[0]:
+                best = (joins, s)
+    if lo_first:
+        seq = ([e] if own else []) + first + best[1]
         start = HALF - own
         q_at, q_from = 0, o_end - HALF
-        lo_first = True
+        base = (start, start + HALF)
+    else:
+        seq = best[1] + first[::-1] + [e]
+        start = (own - NCOL) % 16
+        q_at, q_from = start + NCOL - own, off(cnt, e, e)
+        base = (start + HALF, start)
     pos, p = {}, start
     for j in seq:
         pos[j] = p
         p += cnt[j][e]
-    base = (start, start + HALF) if lo_first else (start + HALF, start)
     group = {j: 0 if j in first or j == cut else 1 for j in eng}
     need = [sum(2 * eng[j] for j in eng if group[j] == h) for h in (0, 1)]
+    block = [j for j in seq if j in direct or j == e]
     return {"pos": pos, "start": start, "base": base, "group": group, "need": need, "own": own,
-            "q_at": q_at, "q_from": q_from, "seq": seq}
+            "q_at": q_at, "q_from": q_from, "seq": seq, "direct": direct,
+            "block": (pos[block[0]], pos[block[-1]] + cnt[block[-1]][e])}
 
 
-def gate_targets(T, roads, lays, j):
-    by = {"g0": [(h, T.gd[:, :]) for h in sorted(roads[j]["gates"])]}
-    for e in range(NR):
-        if j in lays[e]["group"] and e not in roads[j]["gates"].values():
-            by.setdefault("g%d" % lays[e]["group"][j], []).append((T.cores[e], T.gl[j]))
-    return by
-
-
-def send_gates(g, core, T, topo, by):
-    k = ENG_OFF // len(by)
-    everyone = [c for name in by for c, _ in by[name]]
-    trs = []
-    for i, name in enumerate(sorted(by)):
-        ids = []
-        for c, _ in by[name]:
-            rid, pid, _ = topo.addr(c)
-            ids.append(DstId(rid=rid, pnc=pid))
-        trs.append(RemoteDMATransfer(dst_ids=ids, dma_engine_mask=engines(topo, core, everyone, k, i),
-                                     remote_sem=T.sem[name], srcs=[T.gd[:, :]], dsts=[d for _, d in by[name]]))
-    g.remote_dma_fused(trs, local_sem=T.sem.sent)
-    return k * len(by)
-
-
-def send_runs(g, core, T, topo, cnt, lays, j, dests, kind, src, shift):
-    k = ENG_OFF // len(dests)
-    parts = []
-    for i, e in enumerate(dests):
-        lay = lays[e]
-        n, o, p = cnt[j][e], off(cnt, j, e) - shift, lay["pos"][j]
-        if kind == 0:
-            dst, s = T.L[:, p:p + n].bitcast(dt.uint8), src[:, o:o + n].bitcast(dt.uint8)
-        else:
-            dst, s = T.P[:, p:p + n], src[:, o:o + n]
-        parts.append((T.cores[e], dst, s, T.sem["a%d" % lay["group"][j]], engines(topo, core, [T.cores[e]], k, i)))
-    send(g, T, topo, parts)
-    return k * len(dests)
+def send_gates(g, core, T, topo, k, sem, targets):
+    ids = []
+    for c, _ in targets:
+        rid, pid, _ = topo.addr(c)
+        ids.append(DstId(rid=rid, pnc=pid))
+    m = engines(topo, core, [c for c, _ in targets], k)
+    g.remote_dma_fused([RemoteDMATransfer(dst_ids=ids, dma_engine_mask=m, remote_sem=sem, srcs=[T.gd[:, :]],
+                                          dsts=[d for _, d in targets])], local_sem=T.sem.sent)
+    return k
 
 
 def send(g, T, topo, parts):
@@ -194,8 +184,24 @@ def send(g, T, topo, parts):
     g.remote_dma_fused(trs, local_sem=T.sem.sent)
 
 
+def send_runs(g, core, T, topo, cnt, lays, j, dests, kind, src, shift):
+    k = ENG // len(dests)
+    parts = []
+    for i, e in enumerate(dests):
+        lay = lays[e]
+        n, o, p = cnt[j][e], off(cnt, j, e) - shift, lay["pos"][j]
+        if kind == 0:
+            dst, s = T.L[:, p:p + n].bitcast(dt.uint8), src[:, o:o + n].bitcast(dt.uint8)
+        else:
+            dst, s = T.P[:, p:p + n], src[:, o:o + n]
+        parts.append((T.cores[e], dst, s, T.sem["a%d" % lay["group"][j]], engines(topo, core, [T.cores[e]], k, i)))
+    send(g, T, topo, parts)
+    return k * len(dests)
+
+
 def relay(g, core, T, topo, r, kind):
-    k = ENG_RELAY // len(r["groups"])
+    n = len(r["groups"])
+    k = ENG // n
     parts = []
     for i, pair in enumerate(r["who"]):
         a, b = r["wins"][i]
@@ -203,9 +209,9 @@ def relay(g, core, T, topo, r, kind):
             dst, s = T.fc[:, 0:b - a].bitcast(dt.uint8), T.xq[:, a:b].bitcast(dt.uint8)
         else:
             dst, s = T.fs[:, 0:b - a], T.xs[:, a:b]
-        parts.append((pair[kind], dst, s, T.sem.fcs, engines(topo, core, [pair[kind]], k, i)))
+        parts.append((pair[kind], dst, s, T.sem.fcs, engines(topo, core, [pair[kind]], k, i + kind * n)))
     send(g, T, topo, parts)
-    return k * len(parts)
+    return k * n
 
 
 def rank_program(g, core, T, topo):
@@ -224,11 +230,10 @@ def rank_program(g, core, T, topo):
 
 def helper_core(g, core, T, topo, cnt, roads, lays, j, k, kind):
     r = roads[j]
-    e = r["gates"][core]
-    g.wait_ge(T.sem.g0, ENG_OFF // len(gate_targets(T, roads, lays, j)))
-    total = send_gates(g, core, T, topo, {"g%d" % lays[e]["group"][j]: [(T.cores[e], T.gl[j])]})
+    g.wait_ge(T.sem.gh, ENG_GH)
+    total = send_gates(g, core, T, topo, ENG, T.sem.gf, [(T.cores[r["gates"][core]], T.gl[j])])
     src = T.fc if kind == 0 else T.fs
-    g.wait_ge(T.sem.fcs, ENG_RELAY // len(r["groups"]))
+    g.wait_ge(T.sem.fcs, ENG // len(r["groups"]))
     for dests in r["calls"][k]:
         total += send_runs(g, core, T, topo, cnt, lays, j, dests, kind, src, r["wins"][k][0])
     g.wait_ge(T.sem.sent, total)
@@ -257,7 +262,8 @@ def rank_core(g, core, T, topo, cnt, roads, lays, rank):
     V.quantize_mx(T.w2q[:, :], T.w2s[:, :], T.w2t[:, :]).then_inc(S.qw2, 1)
 
     g.wait_ge(S.ldg, 16)
-    total = send_gates(g, core, T, topo, gate_targets(T, roads, lays, rank))
+    total = send_gates(g, core, T, topo, ENG_GH, S.gh, [(h, T.gd[:, :]) for h in sorted(r["gates"])])
+    total += send_gates(g, core, T, topo, ENG, S.gn, [(T.cores[e], T.gl[rank]) for e in r["direct"]])
     g.wait_ge(S.qx, 1)
     total += relay(g, core, T, topo, r, 0)
     total += relay(g, core, T, topo, r, 1)
@@ -265,27 +271,31 @@ def rank_core(g, core, T, topo, cnt, roads, lays, rank):
         total += send_runs(g, core, T, topo, cnt, lays, rank, [e], 0, T.xq, 0)
         total += send_runs(g, core, T, topo, cnt, lays, rank, [e], 1, T.xs, 0)
 
-    for h, q in ((0, Y), (1, A)):
-        srcs = sorted(j for j in lay["group"] if lay["group"][j] == h)
-        n = 0
-        if h == 0 and own:
-            p, o = lay["pos"][rank] - start, off(cnt, rank, rank)
-            q.dma_start(T.gr[0:1, p:p + own], T.gt[0:1, o:o + own]).then_inc(S["lg%d" % h], 16)
-            n += 16
-        if srcs:
-            adds = [ENG_OFF if rank in roads[j]["gates"].values() else ENG_OFF // len(gate_targets(T, roads, lays, j))
-                    for j in srcs]
-            q.wait_ge(S["g%d" % h], sum(adds))
-        for j in srcs:
+    if own:
+        p, o = lay["pos"][rank] - start, off(cnt, rank, rank)
+        Y.dma_start(T.gr[0:1, p:p + own], T.gt[0:1, o:o + own]).then_inc(S.lgn, 16)
+    near = lay["direct"]
+    far = [j for j in lay["group"] if j not in near]
+    for q, js, sem, done, n in ((Y, near, S.gn, S.lgn, len(near)), (A, far[0::2], S.gf, S.lgf, len(far)),
+                                (Y, far[1::2], S.gf, S.lgf, len(far))):
+        if js:
+            q.wait_ge(sem, ENG * n)
+        for j in js:
             p, o, w = lay["pos"][j] - start, off(cnt, j, rank), cnt[j][rank]
-            q.dma_start(T.gr[0:1, p:p + w], T.gl[j, o // 2:(o + w) // 2, :]).then_inc(S["lg%d" % h], 16)
-            n += 16
+            q.dma_start(T.gr[0:1, p:p + w], T.gl[j, o // 2:(o + w) // 2, :]).then_inc(done, 16)
+    n0, n1 = lay["block"][0] - start, lay["block"][1] - start
+    g.wait_ge(S.lgn, 16 * (len(near) + (1 if own else 0)))
+    g.partition_broadcast(T.G[:, n0:n1], T.gr[0:1, n0:n1], 128).then_inc(S.bg, 1)
+    g.wait_ge(S.lgf, 16 * len(far))
+    spread = [1, 1]
     for h in (0, 1):
-        n = 16 * sum(1 for j in lay["seq"] if lay["group"].get(j, 0) == h)
         c = lay["base"][h] - start
-        if n:
-            g.wait_ge(S["lg%d" % h], n)
-        g.partition_broadcast(T.G[:, c:c + HALF], T.gr[0:1, c:c + HALF], 128).then_inc(S["bg%d" % h], 1)
+        for a, b in ((c, min(c + HALF, n0)), (max(c, n1), c + HALF)):
+            if a < b:
+                g.partition_broadcast(T.G[:, a:b], T.gr[0:1, a:b], 128).then_inc(S.bg, 1)
+                spread[1] += 1
+                if h == 0:
+                    spread[0] += 1
 
     PE.wait_ge(S.qw1, 1)
     if own:
@@ -307,14 +317,19 @@ def rank_core(g, core, T, topo, cnt, roads, lays, rank):
     for h in (0, 1):
         c = lay["base"][h] - start
         hb = T["h%d" % h]
-        V.wait_ge(S["bg%d" % h], 1)
+        V.wait_ge(S.bg, spread[h])
         for b in range(4):
             z = 512 * (4 * h + b)
             V.wait_ge(S.mm, 4 * h + b + 1)
             V.tensor_tensor(hb[:, b:512:4], T.zp[:, z:z + HALF], T.G[:, c:c + HALF], AluOpType.mult).then_inc(S.tt, 1)
-        V.wait_ge(S.tt, 4 * h + 4)
-        V.tensor_scalar(hb[:, :], hb[:, :], 0.0, 2.0 ** -5, AluOpType.max, AluOpType.mult).then_inc(S.rl, 1)
-        V.wait_ge(S.rl, h + 1)
+        for b in range(2):
+            A.wait_ge(S.tt, 4 * h + b + 1)
+            A.activation(hb[:, b:512:4], hb[:, b:512:4], ActivationFunctionType.Relu, scale=2.0 ** -5).then_inc(S.ra, 1)
+        for b in range(2, 4):
+            V.wait_ge(S.tt, 4 * h + b + 1)
+            V.tensor_scalar(hb[:, b:512:4], hb[:, b:512:4], 0.0, 2.0 ** -5, AluOpType.max, AluOpType.mult).then_inc(S.rv, 1)
+        V.wait_ge(S.ra, 2 * h + 2)
+        V.wait_ge(S.rv, 2 * h + 2)
         V.quantize_mx(T["hq%d" % h][:, :], T["hs%d" % h][:, :], hb[:, :]).then_inc(S["qh%d" % h], 1)
 
     ypos, p = {}, 0

@@ -36,11 +36,13 @@ SCRATCH = {
 SEMAPHORES = ["ldx", "ldg", "ldw1", "ldw2", "qx", "qo", "qw1", "qw2", "sent",
               "gh", "fcs",
               "gn", "gf", "a0", "a1",
-              "lgn", "lgf", "bg",
-              "mm", "tt", "rv", "ra", "qh0", "qh1", "my0", "my1", "cp", "st"]
+              "gq", "lgn", "lgf", "bg",
+              "mm", "tt", "rv0", "rv1", "ra0", "ra1", "qh0", "qh1", "my0", "my1", "cp", "st"]
 
 ENG = 8
 ENG_GH = 1
+ENG_GF = 4
+ENG_W = (16, 8)
 
 
 def off(cnt, j, e):
@@ -97,12 +99,12 @@ def arrivals(roads, cnt, e):
             continue
         r = roads[j]
         if e in r["near"]:
-            out.append((r["near"].index(e), j, ENG))
+            out.append((r["near"].index(e), j, 2 * ENG))
         else:
             for calls in r["calls"]:
                 for i, c in enumerate(calls):
                     if e in c:
-                        out.append((2 + i, j, ENG // len(c)))
+                        out.append((2 + i, j, 2 * (ENG // len(c))))
     return sorted(out)
 
 
@@ -113,7 +115,7 @@ def orders(js):
 def layout(roads, cnt, e):
     own = cnt[e][e]
     arr = arrivals(roads, cnt, e)
-    eng = {j: k for _, j, k in arr}
+    adds = {j: k for _, j, k in arr}
     first, cut, fill = [], None, own
     rest = [j for _, j, _ in arr]
     while fill < HALF:
@@ -123,20 +125,26 @@ def layout(roads, cnt, e):
             first.append(j)
         else:
             cut = j
-    direct = [j for j in eng if e in roads[j]["direct"]]
-    mid = [] if cut is None else [cut]
+    direct = [j for j in adds if e in roads[j]["direct"]]
     ranks = [j for j in range(NR) if cnt[j][e]]
     nxt = {a: b for a, b in zip(ranks, ranks[1:])}
     o_end = off(cnt, e, e + 1)
     lo_first = not (own and o_end < HALF)
-    first.sort(key=lambda j: (j not in direct, j))
+    ways = [(first, cut, rest)]
+    near = sorted((j for j in adds if e in roads[j]["near"]), key=lambda j: -cnt[j][e])
+    if own + sum(cnt[j][e] for j in near[1:]) < HALF < own + sum(cnt[j][e] for j in near):
+        ways.append((near[1:], near[0], [j for j in adds if j not in near]))
     best = None
-    for a in orders([j for j in rest if j in direct]):
-        for b in orders([j for j in rest if j not in direct]):
-            s = mid + a + b if lo_first else b + a + mid
-            joins = sum(1 for i, j in zip(s, s[1:]) if nxt.get(i) == j)
-            if best is None or joins > best[0]:
-                best = (joins, s)
+    for f, c, r in ways:
+        mid = [] if c is None else [c]
+        for a in orders([j for j in r if j in direct]):
+            for b in orders([j for j in r if j not in direct]):
+                s = mid + a + b if lo_first else b + a + mid
+                pieces = len(s) - sum(1 for i, j in zip(s, s[1:]) if nxt.get(i) == j)
+                if best is None or pieces < best[0]:
+                    best = (pieces, s, f, c)
+    first, cut = best[2], best[3]
+    first.sort(key=lambda j: (j not in direct, j))
     if lo_first:
         seq = ([e] if own else []) + first + best[1]
         start = HALF - own
@@ -151,8 +159,8 @@ def layout(roads, cnt, e):
     for j in seq:
         pos[j] = p
         p += cnt[j][e]
-    group = {j: 0 if j in first or j == cut else 1 for j in eng}
-    need = [sum(2 * eng[j] for j in eng if group[j] == h) for h in (0, 1)]
+    group = {j: 0 if j in first or j == cut else 1 for j in adds}
+    need = [sum(adds[j] for j in adds if group[j] == h) for h in (0, 1)]
     block = [j for j in seq if j in direct or j == e]
     return {"pos": pos, "start": start, "base": base, "group": group, "need": need, "own": own,
             "q_at": q_at, "q_from": q_from, "seq": seq, "direct": direct,
@@ -201,7 +209,7 @@ def send_runs(g, core, T, topo, cnt, lays, j, dests, kind, src, shift):
 
 def relay(g, core, T, topo, r, kind):
     n = len(r["groups"])
-    k = ENG // n
+    k = ENG_W[kind] // n
     parts = []
     for i, pair in enumerate(r["who"]):
         a, b = r["wins"][i]
@@ -231,9 +239,9 @@ def rank_program(g, core, T, topo):
 def helper_core(g, core, T, topo, cnt, roads, lays, j, k, kind):
     r = roads[j]
     g.wait_ge(T.sem.gh, ENG_GH)
-    total = send_gates(g, core, T, topo, ENG, T.sem.gf, [(T.cores[r["gates"][core]], T.gl[j])])
+    total = send_gates(g, core, T, topo, ENG_GF, T.sem.gf, [(T.cores[r["gates"][core]], T.gl[j])])
     src = T.fc if kind == 0 else T.fs
-    g.wait_ge(T.sem.fcs, ENG // len(r["groups"]))
+    g.wait_ge(T.sem.fcs, ENG_W[kind] // len(r["groups"]))
     for dests in r["calls"][k]:
         total += send_runs(g, core, T, topo, cnt, lays, j, dests, kind, src, r["wins"][k][0])
     g.wait_ge(T.sem.sent, total)
@@ -246,8 +254,8 @@ def rank_core(g, core, T, topo, cnt, roads, lays, rank):
     own, start = lay["own"], lay["start"]
     V, A, Y, PE = g.vector, g.scalar, g.sync, g.tensor
 
+    Y.dma_start(T.gd[:, :], T.gt[0:1, :]).then_inc(S.ldg, 16)
     Y.dma_start(T.xt[:, :], T.x[:, :]).then_inc(S.ldx, 16)
-    A.dma_start(T.gd[:, :], T.gt[0:1, :]).then_inc(S.ldg, 16)
     Y.dma_start(T.w1t[:, :], T.w1[:, :]).then_inc(S.ldw1, 16)
     Y.dma_start(T.w2t[:, :], T.w2[:, :]).then_inc(S.ldw2, 16)
 
@@ -267,35 +275,45 @@ def rank_core(g, core, T, topo, cnt, roads, lays, rank):
     g.wait_ge(S.qx, 1)
     total += relay(g, core, T, topo, r, 0)
     total += relay(g, core, T, topo, r, 1)
-    for e in r["near"]:
+    for i, e in enumerate(r["near"]):
+        if i == 1:
+            g.wait_ge(S.gq, 1)
         total += send_runs(g, core, T, topo, cnt, lays, rank, [e], 0, T.xq, 0)
         total += send_runs(g, core, T, topo, cnt, lays, rank, [e], 1, T.xs, 0)
+
+    near = lay["direct"]
+    far = [j for j in lay["group"] if j not in near]
+
+    def pick(q, js, done):
+        for j in js:
+            p, o, w = lay["pos"][j] - start, off(cnt, j, rank), cnt[j][rank]
+            q.dma_start(T.gr[0:1, p:p + w], T.gl[j, o // 2:(o + w) // 2, :]).then_inc(done, 16)
 
     if own:
         p, o = lay["pos"][rank] - start, off(cnt, rank, rank)
         Y.dma_start(T.gr[0:1, p:p + own], T.gt[0:1, o:o + own]).then_inc(S.lgn, 16)
-    near = lay["direct"]
-    far = [j for j in lay["group"] if j not in near]
-    for q, js, sem, done, n in ((Y, near, S.gn, S.lgn, len(near)), (A, far[0::2], S.gf, S.lgf, len(far)),
-                                (Y, far[1::2], S.gf, S.lgf, len(far))):
+    Y.wait_ge(S.gn, ENG * len(near))
+    pick(Y, near, S.lgn)
+    if len(r["near"]) > 1:
+        Y.sem_inc(S.gq, 1)
+    for q, js in ((A, far[0::2]), (Y, far[1::2])):
         if js:
-            q.wait_ge(sem, ENG * n)
-        for j in js:
-            p, o, w = lay["pos"][j] - start, off(cnt, j, rank), cnt[j][rank]
-            q.dma_start(T.gr[0:1, p:p + w], T.gl[j, o // 2:(o + w) // 2, :]).then_inc(done, 16)
+            q.wait_ge(S.gf, ENG_GF * len(far))
+            pick(q, js, S.lgf)
     n0, n1 = lay["block"][0] - start, lay["block"][1] - start
     g.wait_ge(S.lgn, 16 * (len(near) + (1 if own else 0)))
-    g.partition_broadcast(T.G[:, n0:n1], T.gr[0:1, n0:n1], 128).then_inc(S.bg, 1)
-    g.wait_ge(S.lgf, 16 * len(far))
-    spread = [1, 1]
-    for h in (0, 1):
-        c = lay["base"][h] - start
-        for a, b in ((c, min(c + HALF, n0)), (max(c, n1), c + HALF)):
-            if a < b:
-                g.partition_broadcast(T.G[:, a:b], T.gr[0:1, a:b], 128).then_inc(S.bg, 1)
-                spread[1] += 1
-                if h == 0:
-                    spread[0] += 1
+    spread, done = [1, 1], 0
+    for direct in (True, False):
+        if not direct:
+            g.wait_ge(S.lgf, 16 * len(far))
+        for h in (0, 1):
+            c = lay["base"][h] - start
+            cuts = ((max(c, n0), min(c + HALF, n1)),) if direct else ((c, min(c + HALF, n0)), (max(c, n1), c + HALF))
+            for a, b in cuts:
+                if a < b:
+                    g.partition_broadcast(T.G[:, a:b], T.gr[0:1, a:b], 128).then_inc(S.bg, 1)
+                    done += 1
+                    spread[h] = done
 
     PE.wait_ge(S.qw1, 1)
     if own:
@@ -314,23 +332,41 @@ def rank_core(g, core, T, topo, cnt, roads, lays, rank):
         PE.matmul_mx(T.zp[:, 2048 * h:2048 * h + HALF], T.w2q[:, :], T.w2s[:, :],
                      T["hq%d" % h][:, :], T["hs%d" % h][:, :], True, True).then_inc(S["my%d" % h], 1)
 
-    for h in (0, 1):
-        c = lay["base"][h] - start
-        hb = T["h%d" % h]
+    def mult(h):
         V.wait_ge(S.bg, spread[h])
         for b in range(4):
-            z = 512 * (4 * h + b)
+            c, z = lay["base"][h] - start, 512 * (4 * h + b)
             V.wait_ge(S.mm, 4 * h + b + 1)
-            V.tensor_tensor(hb[:, b:512:4], T.zp[:, z:z + HALF], T.G[:, c:c + HALF], AluOpType.mult).then_inc(S.tt, 1)
-        for b in range(2):
-            A.wait_ge(S.tt, 4 * h + b + 1)
-            A.activation(hb[:, b:512:4], hb[:, b:512:4], ActivationFunctionType.Relu, scale=2.0 ** -5).then_inc(S.ra, 1)
-        for b in range(2, 4):
-            V.wait_ge(S.tt, 4 * h + b + 1)
-            V.tensor_scalar(hb[:, b:512:4], hb[:, b:512:4], 0.0, 2.0 ** -5, AluOpType.max, AluOpType.mult).then_inc(S.rv, 1)
-        V.wait_ge(S.ra, 2 * h + 2)
-        V.wait_ge(S.rv, 2 * h + 2)
-        V.quantize_mx(T["hq%d" % h][:, :], T["hs%d" % h][:, :], hb[:, :]).then_inc(S["qh%d" % h], 1)
+            V.tensor_tensor(T["h%d" % h][:, b:512:4], T.zp[:, z:z + HALF], T.G[:, c:c + HALF],
+                            AluOpType.mult).then_inc(S.tt, 1)
+
+    def clip(h, by_scalar):
+        for b in range(4):
+            v = T["h%d" % h][:, b:512:4]
+            if b < by_scalar:
+                A.wait_ge(S.tt, 4 * h + b + 1)
+                A.activation(v, v, ActivationFunctionType.Relu, scale=2.0 ** -5).then_inc(S["ra%d" % h], 1)
+            else:
+                V.wait_ge(S.tt, 4 * h + b + 1)
+                V.tensor_scalar(v, v, 0.0, 2.0 ** -5, AluOpType.max, AluOpType.mult).then_inc(S["rv%d" % h], 1)
+
+    def pack(h, by_scalar):
+        V.wait_ge(S["ra%d" % h], by_scalar)
+        if by_scalar < 4:
+            V.wait_ge(S["rv%d" % h], 4 - by_scalar)
+        V.quantize_mx(T["hq%d" % h][:, :], T["hs%d" % h][:, :], T["h%d" % h][:, :]).then_inc(S["qh%d" % h], 1)
+
+    if n1 - n0 < HALF:
+        for h in (0, 1):
+            mult(h)
+            clip(h, 4)
+        for h in (0, 1):
+            pack(h, 4)
+    else:
+        for h in (0, 1):
+            mult(h)
+            clip(h, 3)
+            pack(h, 3)
 
     ypos, p = {}, 0
     for j in range(NR):

from concourse.bass import DstId, RemoteDMATransfer
from concourse.mybir import dt, AluOpType, ActivationFunctionType

NR = 7
NCOL = 256
HALF = 128
LW = 400

SCRATCH = {
    "xt": ("sbuf", [128, 4 * NCOL], "bfloat16"),
    "w1t": ("sbuf", [128, 2048], "bfloat16"),
    "w2t": ("sbuf", [128, 512], "bfloat16"),
    "xq": ("sbuf", [128, NCOL], "float8_e4m3fn_x4"),
    "xs": ("sbuf", [128, NCOL], "uint8"),
    "w1q": ("sbuf", [128, 512], "float8_e4m3fn_x4"),
    "w1s": ("sbuf", [128, 512], "uint8"),
    "w2q": ("sbuf", [128, 128], "float8_e4m3fn_x4"),
    "w2s": ("sbuf", [128, 128], "uint8"),
    "fc": ("sbuf", [128, NCOL], "float8_e4m3fn_x4"),
    "fs": ("sbuf", [128, NCOL], "uint8"),
    "L": ("sbuf", [128, LW], "float8_e4m3fn_x4"),
    "P": ("sbuf", [128, LW], "uint8"),
    "gd": ("dram", [128, 2], "bfloat16"),
    "gl": ("dram", [NR, 128, 2], "bfloat16"),
    "gr": ("sbuf", [128, NCOL], "bfloat16"),
    "G": ("sbuf", [128, NCOL], "bfloat16"),
    "h0": ("sbuf", [128, 512], "bfloat16"),
    "h1": ("sbuf", [128, 512], "bfloat16"),
    "hq0": ("sbuf", [128, 128], "float8_e4m3fn_x4"),
    "hq1": ("sbuf", [128, 128], "float8_e4m3fn_x4"),
    "hs0": ("sbuf", [128, 128], "uint8"),
    "hs1": ("sbuf", [128, 128], "uint8"),
    "ys": ("sbuf", [128, NCOL], "float32"),
    "zp": ("psum", [128, 512 * 8], "float32"),
}
SEMAPHORES = ["ldx", "ldg", "ldw1", "ldw2", "qx", "qo", "qw1", "qw2", "sent",
              "gh", "fcs",
              "gn", "gf", "a0", "a1",
              "gq", "lgn", "lgf", "bg",
              "mm", "tt", "rv0", "rv1", "ra0", "ra1", "qh0", "qh1", "my0", "my1", "cp", "st"]

ENG = 8
ENG_GH = 1
ENG_GF = 4
ENG_W = (16, 8)


def off(cnt, j, e):
    return sum(cnt[j][:e])


def engines(topo, src, dsts, k, part=0):
    m = -1
    for d in dsts:
        m &= topo.mask(src, d)
    bits = [i for i in range(m.bit_length()) if (m >> i) & 1]
    return sum(1 << i for i in bits[part * k:part * k + k])


def plan(T, topo):
    cnt, cores = T.tables["CNT"], T.cores
    roads = []
    for j in range(NR):
        me = cores[j]
        dests = [e for e in range(NR) if e != j and cnt[j][e]]
        near = [e for e in dests if topo.may_write(me, cores[e])]
        far = [e for e in dests if e not in near]
        near.sort(key=lambda e: -cnt[j][e])
        mates = [c for c in range(me - 8, me + 8)
                 if c >= 0 and c != me and topo.chip(c) == topo.chip(me) and all(topo.may_write(c, cores[e]) for e in far)]
        here = [c for c in mates if topo.die(c) == topo.die(me)]
        there = [c for c in mates if topo.die(c) != topo.die(me)]
        groups = [far[:2], far[2:]] if len(far) > 2 else [far]
        gates = {}
        who = []
        for k, grp in enumerate(groups):
            who.append((here[k], there[k]))
            gates[here[k]] = grp[0]
            gates[there[k]] = grp[1]
        direct = list(near)
        if len(near) > 2:
            groups[0] = groups[0] + [near.pop()]
        wins = [(min(off(cnt, j, e) for e in grp), max(off(cnt, j, e + 1) for e in grp)) for grp in groups]
        w = max(b - a for a, b in wins)
        wins = [(min(a, NCOL - w), min(a, NCOL - w) + w) for a, b in wins]
        calls = []
        for grp in groups:
            widths = sorted(set(cnt[j][e] for e in grp), reverse=True)
            calls.append([[e for e in grp if cnt[j][e] == n] for n in widths])
        roads.append({"near": near, "groups": groups, "who": who, "gates": gates, "direct": direct, "wins": wins,
                      "calls": calls})
    return roads


def arrivals(roads, cnt, e):
    out = []
    for j in range(NR):
        if j == e or not cnt[j][e]:
            continue
        r = roads[j]
        if e in r["near"]:
            out.append((r["near"].index(e), j, 2 * ENG))
        else:
            for calls in r["calls"]:
                for i, c in enumerate(calls):
                    if e in c:
                        out.append((2 + i, j, 2 * (ENG // len(c))))
    return sorted(out)


def orders(js):
    return [[]] if not js else [[j] + o for j in js for o in orders([i for i in js if i != j])]


def layout(roads, cnt, e):
    own = cnt[e][e]
    arr = arrivals(roads, cnt, e)
    adds = {j: k for _, j, k in arr}
    first, cut, fill = [], None, own
    rest = [j for _, j, _ in arr]
    while fill < HALF:
        j = rest.pop(0)
        fill += cnt[j][e]
        if fill <= HALF:
            first.append(j)
        else:
            cut = j
    direct = [j for j in adds if e in roads[j]["direct"]]
    ranks = [j for j in range(NR) if cnt[j][e]]
    nxt = {a: b for a, b in zip(ranks, ranks[1:])}
    o_end = off(cnt, e, e + 1)
    lo_first = not (own and o_end < HALF)
    ways = [(first, cut, rest)]
    near = sorted((j for j in adds if e in roads[j]["near"]), key=lambda j: -cnt[j][e])
    if own + sum(cnt[j][e] for j in near[1:]) < HALF < own + sum(cnt[j][e] for j in near):
        ways.append((near[1:], near[0], [j for j in adds if j not in near]))
    best = None
    for f, c, r in ways:
        mid = [] if c is None else [c]
        for a in orders([j for j in r if j in direct]):
            for b in orders([j for j in r if j not in direct]):
                s = mid + a + b if lo_first else b + a + mid
                pieces = len(s) - sum(1 for i, j in zip(s, s[1:]) if nxt.get(i) == j)
                if best is None or pieces < best[0]:
                    best = (pieces, s, f, c)
    first, cut = best[2], best[3]
    first.sort(key=lambda j: (j not in direct, j))
    if lo_first:
        seq = ([e] if own else []) + first + best[1]
        start = HALF - own
        q_at, q_from = 0, o_end - HALF
        base = (start, start + HALF)
    else:
        seq = best[1] + first[::-1] + [e]
        start = (own - NCOL) % 16
        q_at, q_from = start + NCOL - own, off(cnt, e, e)
        base = (start + HALF, start)
    pos, p = {}, start
    for j in seq:
        pos[j] = p
        p += cnt[j][e]
    group = {j: 0 if j in first or j == cut else 1 for j in adds}
    need = [sum(adds[j] for j in adds if group[j] == h) for h in (0, 1)]
    block = [j for j in seq if j in direct or j == e]
    return {"pos": pos, "start": start, "base": base, "group": group, "need": need, "own": own,
            "q_at": q_at, "q_from": q_from, "seq": seq, "direct": direct,
            "block": (pos[block[0]], pos[block[-1]] + cnt[block[-1]][e])}


def send_gates(g, core, T, topo, k, sem, targets):
    ids = []
    for c, _ in targets:
        rid, pid, _ = topo.addr(c)
        ids.append(DstId(rid=rid, pnc=pid))
    m = engines(topo, core, [c for c, _ in targets], k)
    g.remote_dma_fused([RemoteDMATransfer(dst_ids=ids, dma_engine_mask=m, remote_sem=sem, srcs=[T.gd[:, :]],
                                          dsts=[d for _, d in targets])], local_sem=T.sem.sent)
    return k


def send(g, T, topo, parts):
    if len(parts) == 1:
        c, dst, s, sem, m = parts[0]
        rid, pid, _ = topo.addr(c)
        g.remote_dma(dst, s, sem, T.sem.sent, pid, rid, m)
        return
    trs = []
    for c, dst, s, sem, m in parts:
        rid, pid, _ = topo.addr(c)
        trs.append(RemoteDMATransfer(dst_ids=[DstId(rid=rid, pnc=pid)], dma_engine_mask=m, remote_sem=sem,
                                     srcs=[s], dsts=[dst]))
    g.remote_dma_fused(trs, local_sem=T.sem.sent)


def send_runs(g, core, T, topo, cnt, lays, j, dests, kind, src, shift):
    k = ENG // len(dests)
    parts = []
    for i, e in enumerate(dests):
        lay = lays[e]
        n, o, p = cnt[j][e], off(cnt, j, e) - shift, lay["pos"][j]
        if kind == 0:
            dst, s = T.L[:, p:p + n].bitcast(dt.uint8), src[:, o:o + n].bitcast(dt.uint8)
        else:
            dst, s = T.P[:, p:p + n], src[:, o:o + n]
        parts.append((T.cores[e], dst, s, T.sem["a%d" % lay["group"][j]], engines(topo, core, [T.cores[e]], k, i)))
    send(g, T, topo, parts)
    return k * len(dests)


def relay(g, core, T, topo, r, kind):
    n = len(r["groups"])
    k = ENG_W[kind] // n
    parts = []
    for i, pair in enumerate(r["who"]):
        a, b = r["wins"][i]
        if kind == 0:
            dst, s = T.fc[:, 0:b - a].bitcast(dt.uint8), T.xq[:, a:b].bitcast(dt.uint8)
        else:
            dst, s = T.fs[:, 0:b - a], T.xs[:, a:b]
        parts.append((pair[kind], dst, s, T.sem.fcs, engines(topo, core, [pair[kind]], k, i + kind * n)))
    send(g, T, topo, parts)
    return k * n


def rank_program(g, core, T, topo):
    cnt = T.tables["CNT"]
    roads = plan(T, topo)
    lays = [layout(roads, cnt, e) for e in range(NR)]
    rank = T.rank_of(core)
    if rank is not None:
        rank_core(g, core, T, topo, cnt, roads, lays, rank)
        return
    for j in range(NR):
        for k, pair in enumerate(roads[j]["who"]):
            if core in pair:
                helper_core(g, core, T, topo, cnt, roads, lays, j, k, pair.index(core))


def helper_core(g, core, T, topo, cnt, roads, lays, j, k, kind):
    r = roads[j]
    g.wait_ge(T.sem.gh, ENG_GH)
    total = send_gates(g, core, T, topo, ENG_GF, T.sem.gf, [(T.cores[r["gates"][core]], T.gl[j])])
    src = T.fc if kind == 0 else T.fs
    g.wait_ge(T.sem.fcs, ENG_W[kind] // len(r["groups"]))
    for dests in r["calls"][k]:
        total += send_runs(g, core, T, topo, cnt, lays, j, dests, kind, src, r["wins"][k][0])
    g.wait_ge(T.sem.sent, total)


def rank_core(g, core, T, topo, cnt, roads, lays, rank):
    S = T.sem
    r = roads[rank]
    lay = lays[rank]
    own, start = lay["own"], lay["start"]
    V, A, Y, PE = g.vector, g.scalar, g.sync, g.tensor

    Y.dma_start(T.gd[:, :], T.gt[0:1, :]).then_inc(S.ldg, 16)
    Y.dma_start(T.xt[:, :], T.x[:, :]).then_inc(S.ldx, 16)
    Y.dma_start(T.w1t[:, :], T.w1[:, :]).then_inc(S.ldw1, 16)
    Y.dma_start(T.w2t[:, :], T.w2[:, :]).then_inc(S.ldw2, 16)

    V.wait_ge(S.ldx, 16)
    V.quantize_mx(T.xq[:, :], T.xs[:, :], T.xt[:, :]).then_inc(S.qx, 1)
    if own:
        a, c = lay["q_at"], lay["q_from"]
        V.quantize_mx(T.L[:, a:a + HALF], T.P[:, a:a + HALF], T.xt[:, 4 * c:4 * (c + HALF)]).then_inc(S.qo, 1)
    V.wait_ge(S.ldw1, 16)
    V.quantize_mx(T.w1q[:, :], T.w1s[:, :], T.w1t[:, :]).then_inc(S.qw1, 1)
    V.wait_ge(S.ldw2, 16)
    V.quantize_mx(T.w2q[:, :], T.w2s[:, :], T.w2t[:, :]).then_inc(S.qw2, 1)

    g.wait_ge(S.ldg, 16)
    total = send_gates(g, core, T, topo, ENG_GH, S.gh, [(h, T.gd[:, :]) for h in sorted(r["gates"])])
    total += send_gates(g, core, T, topo, ENG, S.gn, [(T.cores[e], T.gl[rank]) for e in r["direct"]])
    g.wait_ge(S.qx, 1)
    total += relay(g, core, T, topo, r, 0)
    total += relay(g, core, T, topo, r, 1)
    for i, e in enumerate(r["near"]):
        if i == 1:
            g.wait_ge(S.gq, 1)
        total += send_runs(g, core, T, topo, cnt, lays, rank, [e], 0, T.xq, 0)
        total += send_runs(g, core, T, topo, cnt, lays, rank, [e], 1, T.xs, 0)

    near = lay["direct"]
    far = [j for j in lay["group"] if j not in near]

    def pick(q, js, done):
        for j in js:
            p, o, w = lay["pos"][j] - start, off(cnt, j, rank), cnt[j][rank]
            q.dma_start(T.gr[0:1, p:p + w], T.gl[j, o // 2:(o + w) // 2, :]).then_inc(done, 16)

    if own:
        p, o = lay["pos"][rank] - start, off(cnt, rank, rank)
        Y.dma_start(T.gr[0:1, p:p + own], T.gt[0:1, o:o + own]).then_inc(S.lgn, 16)
    Y.wait_ge(S.gn, ENG * len(near))
    pick(Y, near, S.lgn)
    if len(r["near"]) > 1:
        Y.sem_inc(S.gq, 1)
    for q, js in ((A, far[0::2]), (Y, far[1::2])):
        if js:
            q.wait_ge(S.gf, ENG_GF * len(far))
            pick(q, js, S.lgf)
    n0, n1 = lay["block"][0] - start, lay["block"][1] - start
    g.wait_ge(S.lgn, 16 * (len(near) + (1 if own else 0)))
    spread, done = [1, 1], 0
    for direct in (True, False):
        if not direct:
            g.wait_ge(S.lgf, 16 * len(far))
        for h in (0, 1):
            c = lay["base"][h] - start
            cuts = ((max(c, n0), min(c + HALF, n1)),) if direct else ((c, min(c + HALF, n0)), (max(c, n1), c + HALF))
            for a, b in cuts:
                if a < b:
                    g.partition_broadcast(T.G[:, a:b], T.gr[0:1, a:b], 128).then_inc(S.bg, 1)
                    done += 1
                    spread[h] = done

    PE.wait_ge(S.qw1, 1)
    if own:
        PE.wait_ge(S.qo, 1)
    for h in (0, 1):
        if lay["need"][h]:
            PE.wait_ge(S["a%d" % h], lay["need"][h])
        c = lay["base"][h]
        for b in range(4):
            z = 512 * (4 * h + b)
            PE.matmul_mx(T.zp[:, z:z + HALF], T.w1q[:, 128 * b:128 * b + 128], T.w1s[:, 128 * b:128 * b + 128],
                         T.L[:, c:c + HALF], T.P[:, c:c + HALF], True, True).then_inc(S.mm, 1)
    PE.wait_ge(S.qw2, 1)
    for h in (0, 1):
        PE.wait_ge(S["qh%d" % h], 1)
        PE.matmul_mx(T.zp[:, 2048 * h:2048 * h + HALF], T.w2q[:, :], T.w2s[:, :],
                     T["hq%d" % h][:, :], T["hs%d" % h][:, :], True, True).then_inc(S["my%d" % h], 1)

    def mult(h):
        V.wait_ge(S.bg, spread[h])
        for b in range(4):
            c, z = lay["base"][h] - start, 512 * (4 * h + b)
            V.wait_ge(S.mm, 4 * h + b + 1)
            V.tensor_tensor(T["h%d" % h][:, b:512:4], T.zp[:, z:z + HALF], T.G[:, c:c + HALF],
                            AluOpType.mult).then_inc(S.tt, 1)

    def clip(h, by_scalar):
        for b in range(4):
            v = T["h%d" % h][:, b:512:4]
            if b < by_scalar:
                A.wait_ge(S.tt, 4 * h + b + 1)
                A.activation(v, v, ActivationFunctionType.Relu, scale=2.0 ** -5).then_inc(S["ra%d" % h], 1)
            else:
                V.wait_ge(S.tt, 4 * h + b + 1)
                V.tensor_scalar(v, v, 0.0, 2.0 ** -5, AluOpType.max, AluOpType.mult).then_inc(S["rv%d" % h], 1)

    def pack(h, by_scalar):
        V.wait_ge(S["ra%d" % h], by_scalar)
        if by_scalar < 4:
            V.wait_ge(S["rv%d" % h], 4 - by_scalar)
        V.quantize_mx(T["hq%d" % h][:, :], T["hs%d" % h][:, :], T["h%d" % h][:, :]).then_inc(S["qh%d" % h], 1)

    if n1 - n0 < HALF:
        for h in (0, 1):
            mult(h)
            clip(h, 4)
        for h in (0, 1):
            pack(h, 4)
    else:
        for h in (0, 1):
            mult(h)
            clip(h, 3)
            pack(h, 3)

    ypos, p = {}, 0
    for j in range(NR):
        ypos[j] = p
        p += cnt[j][rank]
    copies = 0
    for h in (0, 1):
        lo = lay["base"][h]
        segs = []
        for j in lay["seq"]:
            a = max(lay["pos"][j], lo)
            b = min(lay["pos"][j] + cnt[j][rank], lo + HALF)
            if a >= b:
                continue
            to = ypos[j] + a - lay["pos"][j]
            if segs and segs[-1][1] + segs[-1][2] == to:
                segs[-1][2] += b - a
            else:
                segs.append([a - lo, to, b - a])
        (A if h == 0 else V).wait_ge(S["my%d" % h], 1)
        for a, to, n in segs:
            src, dst = T.zp[:, 2048 * h + a:2048 * h + a + n], T.ys[:, to:to + n]
            if h == 0:
                A.activation(dst, src, ActivationFunctionType.Copy).then_inc(S.cp, 1)
            else:
                V.tensor_copy(dst, src).then_inc(S.cp, 1)
            copies += 1
    Y.wait_ge(S.cp, copies)
    Y.dma_start(T.y[:, :], T.ys[:, :]).then_inc(S.st, 16)
    Y.wait_ge(S.st, 16)
    g.wait_ge(S.sent, total)
